import numpy as np, ml_dtypes
CORES = [5,29,101,125,133,157,229,253]
N = 8
BF = ml_dtypes.bfloat16
def gentries(a):
    return np.ascontiguousarray(a.reshape(8, 16, -1).transpose(0, 2, 1)).reshape(8, -1)
def gtable(e):
    e = np.asarray(e); return np.ascontiguousarray(e.reshape(8, -1, 16).transpose(0, 2, 1)).reshape(128, -1).astype(np.int32)
W, NB, R, H = 4096, 8, 4, 5
KAP = (101, 1303, 2717, 3911)
def spot(u, l):
    return ((u * u >> 5) + 37 * u + KAP[l]) & (W - 1)
def figures(x, n):
    return np.take_along_axis(x, n.reshape(8, 1, -1), 2).reshape((8, 16) + n.shape[1:])
def witness(x, w, F):
    w = w.reshape(8, 16, 1, 1, 1)
    for l in range(4):
        h = F.shape[3] >> 1
        a, b = F[:, :, :, 0::2], F[:, :, :, 1::2]
        u = np.add.reduce(w * np.abs(a - b), axis=1) & (W - 1)
        F = figures(x, spot(u, l))
    return F[:, :, :, 0]
def judge(x, w, n):
    F = figures(x, n)
    col = witness(x, w, F); row = witness(x, w, F.transpose(0, 1, 2, 4, 3))
    return col, np.add.reduce(np.abs(col - row), axis=1), np.add.reduce(col, axis=1), np.add.reduce(row, axis=1)
def readings(x, w, n):
    x8 = np.broadcast_to(x, (8, 16, W)); w8 = np.broadcast_to(w, (8, 16))
    return np.ascontiguousarray(witness(x8, w8, figures(x8, n.reshape(8, -1, 16, 1)))[..., 0].transpose(1, 0, 2)).reshape(16, -1)
def parts(rng):
    x = rng.integers(0, 256, (N, 8, 16, W)); w = rng.integers(0, 256, (N, 8, 16)); th = rng.integers(800, 2000, (N, 8, 16))
    return x, w, th, rng.integers(0, W, (N, 8, NB * 256)), rng.integers(0, W, (N, 8, NB * 256))
def pack(x, w, th, b, c):
    return {"xf": np.ascontiguousarray(x.reshape(N, 128, W)).astype(np.float32).astype(BF), "bn": np.stack([gtable(a) for a in b]), "cn": np.stack([gtable(a) for a in c]),
            "wt": np.ascontiguousarray(w.reshape(N, 128, 1)).astype(np.int32), "th": np.ascontiguousarray(th.reshape(N, 128, 1)).astype(np.int32)}
def setup_inputs(rng):
    return pack(*parts(rng))
def setup_inputs_spread(rng):
    x, w, th, b, c = parts(rng)
    s = np.exp2(8.5 * rng.random((N, 8, 1, W))) * (rng.random((N, 8, 1, W)) > 0.0625)
    x = np.minimum((s * rng.random((N, 8, 16, W))).astype(np.int64), 255)
    w = np.minimum(np.exp2(8 * rng.random((N, 8, 16))).astype(np.int64) - rng.integers(0, 2, (N, 8, 16)), 255)
    th = np.minimum(np.exp2(11 * rng.random((N, 8, 16))).astype(np.int64), 4080)
    b = np.minimum((W * rng.random(b.shape) ** 3).astype(np.int64), W - 1); c = np.minimum((W * rng.random(c.shape) ** 2).astype(np.int64), W - 1)
    b[:, 1::2] = W - 1 - b[:, 1::2]; c[:, ::3] = W - 1 - c[:, ::3]
    return pack(x, w, th, b, c)
def setup_inputs_ends(rng):
    x = 255 * rng.integers(0, 2, (N, 8, 16, W)); w = 255 * rng.integers(0, 2, (N, 8, 16)); th = 4080 * rng.integers(0, 2, (N, 8, 16))
    w[:, 0, 0] = 0; w[:, 0, 15] = 255; th[:, 0, 0] = 0; th[:, 0, 15] = 4080
    b, c = [np.where(rng.random((N, 8, NB * 256)) < 0.8, (W - 1) * rng.integers(0, 2, (N, 8, NB * 256)), rng.integers(0, W, (N, 8, NB * 256))) for i in range(2)]
    for g in (2, 5, 7):
        x[:, g] = 255 * rng.integers(0, 2, (N, 1, W)); w[:, g] = 255
    for q in range(0, N - 1, 2): w[q, 7, q] = 0
    for q in range(N):
        for g in (2, 5, 7):
            u = 255 * int(np.add.reduce(w[q, g])) & (W - 1)
            x[q, g, :, 0] = 0; x[q, g, :, W - 1] = 255
            for l in range(4): x[q, g, :, spot(0, l)] = 0
            for l in range(4): x[q, g, :, spot(u, l)] = 255
    bb = b.reshape(N, 8, NB, 16, 16)
    bb[:, 7, :, :, 0] = 0; bb[:, 7, NB - 1] = 0; bb[:, 7, NB - 1, 0, 15] = W - 1; bb[:, 7, NB - 1, 1, 0] = W - 1
    th[:, 7, 15] = 0; th[N - 1, 7, 15] = 4080
    return pack(x, w, th, bb.reshape(N, 8, NB * 256), c)
def setup_inputs_corners(rng):
    x, w, th, b, c = parts(rng)
    for q in range(N):
        for g in range(8):
            k = (g + q) % 8
            if k == 0: w[q, g] = 0
            if k == 1: w[q, g] = 255
            if k == 2: w[q, g] = 16 * rng.integers(1, 16, 16); th[q, g] = 0
            if k == 3: th[q, g] = 4080
            if k == 4: b[q, g] = np.repeat(rng.choice(np.array([0, 1, W - 1, W >> 1]), NB), 256); c[q, g] = rng.permutation(NB * 256) % W
            if k == 5: b[q, g] = np.arange(NB * 256) % W; c[q, g] = W - 1 - b[q, g]
            if k == 6: w[q, g] = 0; w[q, g, 15] = 255
            if k == 7: x[q, g] = 255 * rng.integers(0, 2, (1, W))
    return pack(x, w, th, b, c)
def setup_inputs_full(rng):
    x, w, th, b, c = parts(rng); bb = b.reshape(N, 8, NB, 16, 16); z = spot(0, 3)
    for q in range(N):
        for g in range(8):
            k = (g + q) % 8
            if k < 4: th[q, g] = rng.integers(0, 256, 16)
            if k < 3:
                w[q, g, 0] |= 1; x[q, g, :, z] = rng.integers(240, 256, 16)
                n = rng.integers(0, W, (512, 16)); f = readings(x[q, g], w[q, g], n)
                s = np.add.reduce(f, axis=0); d = np.add.reduce(w[q, g][:, None] * f, axis=0) & (NB - 1)
                for v, p in enumerate(rng.permutation(NB)):
                    turn = k == 1 or (k == 2 and p % 2 == 1)
                    i = int(np.argmax(np.where(d == v, -s if turn else s, -5000)))
                    bb[q, g, p] = n[i][:, None] if turn else rng.integers(0, W, (1, 16))
                    bb[q, g, p, :, 0] = n[i]
            if k == 3:
                w[q, g] = 255; x[q, g, :, z] = 255; x[q, g, rng.permutation(16)[:2 + q], z] = 254
                bb[q, g, :, :, 0] = rng.integers(0, W, (NB, 1))
            if k == 4: x[q, g] = rng.integers(235, 256, (16, W)); w[q, g] = rng.integers(253, 256, 16)
            if k == 7: x[q, g] = rng.integers(246, 256, (16, W)); w[q, g] = rng.integers(240, 256, 16)
            if k == 5 or k == 6:
                e = int(rng.choice(np.array([8, 24, 60, 90])))
                x[q, g] = np.abs(255 * rng.integers(0, 2, (1, W)) - rng.integers(0, e + 1, (16, W))); w[q, g] = rng.integers(240, 256, 16)
        col, D, A, E = judge(x[q], w[q], bb[q])
        i = np.argmax(np.where(D >= 2304, rng.random(D.shape), -1.0), axis=1)
        t = np.take_along_axis(D - (A & 15), i[:, None, :], 1)[:, 0] - rng.integers(0, 2, (8, 16))
        for g in range(8):
            k = (g + q) % 8
            if k > 3: th[q, g] = np.minimum(np.maximum(t[g], 0), 4080)
            if k == 4 or k == 7: th[q, g, ::2] = rng.integers(0, 16, 8)
    return pack(x, w, th, bb.reshape(N, 8, NB * 256), c)
def setup_inputs_ties(rng):
    x, w, th, b, c = parts(rng)
    base = rng.integers(0, 256, (N, 16, 1)); order = np.argsort(rng.random((N, 16, W)), axis=1)
    x[:, 6] = np.take_along_axis(np.ascontiguousarray(np.broadcast_to(base, (N, 16, W))), order, 1)
    x[:, 4, :, 1::2] = x[:, 4, :, 0::2]
    bb = b.reshape(N, 8, NB, 16, 16)
    s = bb[:, 1, ::3].copy(); bb[:, 1, ::3] = np.triu(s) + np.swapaxes(np.triu(s, 1), -1, -2)
    bb[:, 2, :, :, 0] = bb[:, 2, :1, :, 0].copy()
    for q in range(N):
        col, D, A, E = judge(x[q], w[q], bb[q])
        v = np.take_along_axis(D - (A & 15), rng.integers(0, NB, (8, 1, 16)), 1)[:, 0]
        th[q] = np.minimum(np.maximum(v + rng.choice(np.array([-1, 0, 0, 1]), (8, 16)), 0), 4080)
    th[:, 6, 1::2] = 0
    return pack(x, w, th, bb.reshape(N, 8, NB * 256), c)
def check_inputs(d):
    bad = []
    for k, lo, hi in (("xf", 0, 255), ("bn", 0, W - 1), ("cn", 0, W - 1), ("wt", 0, 255), ("th", 0, 4080)):
        v = np.asarray(d[k]).astype(np.float64)
        if not (np.min(v) >= lo and np.max(v) <= hi): bad.append("range of " + k)
        if np.any(v != np.floor(v)): bad.append("whole numbers of " + k)
    return bad
def reference(xf, bn, cn, wt, th):
    x = np.asarray(xf).astype(np.float32).astype(np.int64).reshape(N, 8, 16, W); w = wt.astype(np.int64).reshape(N, 8, 16); lim = th.astype(np.int64).reshape(N, 8, 16)
    b = np.stack([gentries(a) for a in bn]).astype(np.int64).reshape(N, 8, NB, 16, 16)
    c = np.stack([gentries(a) for a in cn]).astype(np.int64).reshape(N, 8, NB, 16, 16)
    cnt = np.zeros((N, 8, NB, 16), np.int64); low = np.tril(np.ones((NB, NB), bool), -1)
    for t in range(R):
        for a in range(N):
            q = (a - H * t) % N
            col, D, A, E = judge(x[a], w[a], b[q])
            qr = D > lim[a][:, None, :] + (A & 15); cnt[a] += qr
            d = np.add.reduce(w[a][:, :, None] * col[:, :, :, 0], axis=1) & (NB - 1)
            act = ~np.any((d[:, :, None] == d[:, None, :]) & low, axis=2)
            for g in range(8):
                for k in np.flatnonzero(act[g]):
                    one, two = b[q, g, k], c[a, g, d[g, k]]
                    j = np.flatnonzero(qr[g, k] & (A[g, k] <= E[g, k])); v = one[:, j]; one[:, j] = two[:, j]; two[:, j] = v
                    j = np.flatnonzero(qr[g, k] & (A[g, k] > E[g, k])); v = one[j]; one[j] = two[j]; two[j] = v
    yb = np.stack([gtable(b[(a - H * (R - 1)) % N].reshape(8, -1)) for a in range(N)]); yc = np.stack([gtable(e.reshape(8, -1)) for e in c])
    return {"yb": yb.astype(np.float32), "yc": yc.astype(np.float32), "yq": np.ascontiguousarray(cnt.transpose(0, 1, 3, 2)).reshape(N, 128, NB).astype(np.float32)}

@@ -1,0 +1,492 @@
+from concourse.mybir import dt, AluOpType, AxisListType, ActivationFunctionType
+
+R, H, N = 4, 5, 8
+KAP = (101, 1303, 2717, 3911)
+PADL = 48
+SHIFT = (1437, 2639, 5, 1151)
+WINS = ((48, 5584), (48, 6784), (0, 4112), (48, 5296))
+
+SCRATCH = {"xt": ("sbuf", [128, 6784], "bfloat16")}
+
+
+def _sb(name, cols, d):
+    SCRATCH[name] = ("sbuf", [128, cols], d)
+
+
+for _n, _c, _d in (("bni", 128, "int32"), ("cni", 128, "int32"), ("wti", 1, "int32"), ("thi", 1, "int32"),
+                   ("ones", 144, "float32"), ("a1", 144, "float32"), ("a2", 144, "float32"), ("p0", 144, "float32"),
+                   ("q0", 144, "float32"), ("idf", 128, "float32"), ("ki", 4, "int32"), ("kf", 4, "float32"),
+                   ("wf", 2, "float32"), ("tht", 2, "int32"), ("thf", 2, "float32"), ("i4", 4, "float32"),
+                   ("i44", 4, "float32"), ("jj", 64, "float32"), ("pcon", 4, "float32"), ("kc", 2, "float32"),
+                   ("pw", 144, "bfloat16"), ("p16", 144, "bfloat16"), ("wb8", 128, "bfloat16"), ("q8", 144, "bfloat16"),
+                   ("idn", 128, "bfloat16"), ("nid", 128, "bfloat16"), ("ob", 128, "bfloat16"), ("nob", 128, "bfloat16"),
+                   ("no16", 128, "bfloat16"), ("lt", 4, "bfloat16"), ("rhi", 64, "bfloat16"), ("rlo", 64, "bfloat16"),
+                   ("win", 256, "float32"), ("ybt", 128, "float32"), ("yqt", 8, "float32")):
+    _sb(_n, _c, _d)
+for _h in (0, 1):
+    for _n, _c, _d in (("f0", 1024, "bfloat16"), ("f1", 1024, "bfloat16"), ("f2", 512, "bfloat16"), ("f3", 256, "bfloat16"),
+                       ("w4", 128, "bfloat16"), ("d0", 1024, "bfloat16"), ("d1", 512, "bfloat16"), ("d2", 256, "bfloat16"),
+                       ("d3", 128, "bfloat16"), ("dw", 64, "bfloat16"), ("ti", 64, "int32"), ("tu", 64, "int32"),
+                       ("tq", 64, "int32"), ("tz", 64, "int32"), ("o0", 64, "uint16"),
+                       ("o1", 32, "uint16"), ("o2", 16, "uint16"), ("o3", 8, "uint16"), ("rr", 12, "int32"),
+                       ("ff", 12, "float32"), ("ds", 1, "float32"), ("de", 1, "float32"), ("eq", 8, "float32"),
+                       ("us", 1, "float32"), ("tt", 1, "float32"), ("s1", 1, "float32"), ("oc", 4, "uint16"),
+                       ("gc", 64, "float32"), ("ai", 64, "int32"), ("am", 64, "int32"), ("a3", 64, "float32"),
+                       ("qq", 64, "bfloat16"), ("mc", 64, "bfloat16"), ("mr", 64, "bfloat16"),
+                       ("ee", 64, "float32"), ("me", 64, "float32"), ("bn2", 64, "float32"), ("qs", 64, "bfloat16"),
+                       ("ch", 64 * R, "uint16"), ("co", 64 * R, "uint16")):
+        _sb(_n + "h%d" % _h, _c, _d)
+    for _n in ("PA", "PB", "PS", "PT"):
+        SCRATCH[_n + "h%d" % _h] = ("psum", [128, 512], "float32")
+
+DMAS = ["lw", "lt", "lb", "lc", "lx", "le", "lf", "ll", "sb0", "sb1", "sc", "sq"]
+SEMAPHORES = ["cv", "ca", "cp", "cg", "snd"] + ["m_" + d for d in DMAS] + \
+             ["ar%d%d" % (t, h) for t in range(1, R) for h in (0, 1)] + ["rl%d%d" % (t, h) for t in range(1, R) for h in (0, 1)]
+
+NENG = 8
+HOP = 5000.0
+CY = 0.95
+AF, AO = ActivationFunctionType, AluOpType
+
+
+def build():
+    ops, track = [], {}
+
+    def add(eng, dur, emit, R_=(), W_=(), tail=0.0, sem=None, after=()):
+        i = len(ops)
+        order, waits = set(), set()
+        for (b, lo, hi), wr in [(x, False) for x in R_] + [(x, True) for x in W_]:
+            ps = b[0] == "P"
+            for (lo2, hi2, j, wr2) in track.get(b, ()):
+                if j == i:
+                    continue
+                e2 = ops[j]["eng"]
+                clash = lo < hi2 and lo2 < hi
+                if ps and e2 != eng:
+                    clash = True
+                elif not (wr or wr2):
+                    clash = False
+                if not clash:
+                    continue
+                order.add(j)
+                if e2 == eng == "p":
+                    continue
+                waits.add(j)
+        for j in after:
+            order.add(j)
+        ops.append({"eng": eng, "dur": dur, "emit": emit, "order": order, "waits": waits, "tail": tail, "sem": sem, "late": set(after)})
+        for (b, lo, hi), wr in [(x, False) for x in R_] + [(x, True) for x in W_]:
+            l = track.setdefault(b, [])
+            if wr:
+                l[:] = [e for e in l if e[2] == i or not (lo <= e[0] and e[1] <= hi)]
+            l.append((lo, hi, i, wr))
+        return i
+
+    def V(n, emit, R_, W_, f=1.0):
+        return add("v", 10 + max(64, n * f) * CY, emit, R_, W_)
+
+    def A(n, emit, R_, W_):
+        return add("a", 20 + max(64, n) * CY, emit, R_, W_)
+
+    def G(n, emit, R_, W_):
+        return add("g", 150 + 2 * n * CY, emit, R_, W_)
+
+    def P(mms, R_, W_):
+        dur = 10 + sum(max(64, m[0]) * 0.42 for m in mms)
+
+        def emit(g, T):
+            for m in mms:
+                last = g.tensor.matmul(m[1](T), m[2](T), m[3](T), m[4], m[5])
+            return last
+        return add("p", dur, emit, R_, W_)
+
+    def D(q, name, out, in_, dur, R_, W_):
+        def emit(g, T):
+            return (g.sync if q == "s" else g.scalar).dma_start(out(T), in_(T))
+        return add(q, 60.0, emit, R_, W_, tail=dur, sem=("m_" + name, 16))
+
+    def full(b):
+        return (b, 0, SCRATCH[b][1][1])
+
+    def val(x, T):
+        return x if x is None or isinstance(x, (int, float)) else x(T)
+
+    def ts(o, oi, a, ai, s1, s2, op0, op1=None):
+        def emit(g, T):
+            if op1 is None:
+                return g.vector.tensor_scalar(T[o][:, oi], T[a][:, ai], val(s1, T), None, op0=op0)
+            return g.vector.tensor_scalar(T[o][:, oi], T[a][:, ai], val(s1, T), val(s2, T), op0=op0, op1=op1)
+        return emit
+
+    def cp(o, oi, a, ai):
+        return lambda g, T: g.vector.tensor_copy(T[o][:, oi], T[a][:, ai])
+
+    def tt(o, oi, a, ai, b, bi, op):
+        return lambda g, T: g.vector.tensor_tensor(T[o][:, oi], T[a][:, ai], T[b][:, bi], op)
+
+    S_ = slice
+    al = S_(None)
+
+    def col(b, c):
+        return lambda T: T[b][:, c:c + 1]
+
+    D("a", "lw", lambda T: T.wti[:], lambda T: T.wt[:], 2000.0, (), (full("wti"),))
+    D("a", "lb", lambda T: T.bni[:], lambda T: T.bn[:], 2200.0, (), (full("bni"),))
+    D("s", "lx", lambda T: T.xt[:, PADL:PADL + 4096], lambda T: T.xf[:], 7500.0, (), (("xt", 48, 4144),))
+    D("a", "lt", lambda T: T.thi[:], lambda T: T.th[:], 2200.0, (), (full("thi"),))
+    D("a", "lc", lambda T: T.cni[:], lambda T: T.cn[:], 2500.0, (), (full("cni"),))
+    D("s", "le", lambda T: T.xt[:, 4144:5584], lambda T: T.xf[:, 0:1440], 9500.0, (), (("xt", 4144, 5584),))
+    D("s", "lf", lambda T: T.xt[:, 5584:6784], lambda T: T.xf[:, 1440:2640], 11500.0, (), (("xt", 5584, 6784),))
+    D("s", "ll", lambda T: T.xt[:, 0:48], lambda T: T.xf[:, 4048:4096], 12000.0, (), (("xt", 0, 48),))
+    V(144, lambda g, T: g.vector.memset(T.ones[:], 1.0), (), (full("ones"),))
+    G(1, lambda g, T: g.iota(T.ki[:, 0:1], [[1, 1]], 0, 1), (), (("ki", 0, 1),))
+    G(128, lambda g, T: g.affine_select(T.idf[:], T.ones[:, 0:128], [[-1, 128]], AO.is_equal, 0.0, 0, 1),
+      (full("ones"),), (full("idf"),))
+    G(144, lambda g, T: g.affine_select(T.a1[:], T.ones[:], [[-16, 9], [0, 16]], AO.is_ge, 0.0, 0, 1),
+      (full("ones"),), (full("a1"),))
+    G(144, lambda g, T: g.affine_select(T.a2[:], T.a1[:], [[16, 9], [0, 16]], AO.is_ge, 0.0, 15, -1),
+      (full("a1"),), (full("a2"),))
+    G(144, lambda g, T: g.affine_select(T.p0[:], T.a2[:], [[0, 9], [1, 16]], AO.is_equal, 0.0, -15, 0),
+      (full("a2"),), (full("p0"),))
+    G(144, lambda g, T: g.affine_select(T.q0[:], T.a2[:], [[0, 36], [1, 4]], AO.is_equal, 0.0, -3, 0),
+      (full("a2"),), (full("q0"),))
+    G(4, lambda g, T: g.iota(T.i4[:], [[1, 4]], 0, 0, allow_small_or_imprecise_dtypes=True), (), (full("i4"),))
+    G(4, lambda g, T: g.iota(T.i44[:], [[4, 4]], 0, 0, allow_small_or_imprecise_dtypes=True), (), (full("i44"),))
+    G(64, lambda g, T: g.iota(T.jj[:], [[1, 16], [0, 4]], 0, 0, allow_small_or_imprecise_dtypes=True), (), (full("jj"),))
+    V(1, cp("wf", S_(0, 1), "wti", al), (full("wti"),), (("wf", 0, 1),))
+    V(1, ts("wf", S_(1, 2), "wti", al, 0.125, None, AO.mult), (full("wti"),), (("wf", 1, 2),))
+    V(1, ts("ki", S_(1, 2), "ki", S_(0, 1), 3, None, AO.bitwise_and), (("ki", 0, 1),), (("ki", 1, 2),))
+    V(1, ts("ki", S_(2, 3), "ki", S_(0, 1), 2, 3, AO.logical_shift_right, AO.bitwise_and), (("ki", 0, 1),), (("ki", 2, 3),))
+    V(1, ts("ki", S_(3, 4), "ki", S_(0, 1), 15, None, AO.bitwise_and), (("ki", 0, 1),), (("ki", 3, 4),))
+    V(3, cp("kf", S_(1, 4), "ki", S_(1, 4)), (("ki", 1, 4),), (("kf", 1, 4),))
+    V(128, cp("idn", al, "idf", al), (full("idf"),), (full("idn"),))
+    V(128, ts("nid", al, "idf", al, -1.0, None, AO.mult), (full("idf"),), (full("nid"),))
+    V(144, ts("pw", al, "p0", al, col("wf", 0), None, AO.mult), (full("p0"), ("wf", 0, 1)), (full("pw"),))
+    V(144, ts("p16", al, "p0", al, 0.0625, None, AO.mult), (full("p0"),), (full("p16"),))
+    V(128, ts("wb8", al, "a2", S_(0, 128), col("wf", 1), None, AO.mult), (full("a2"), ("wf", 1, 2)), (full("wb8"),))
+    V(144, ts("q8", al, "q0", al, col("wf", 1), None, AO.mult), (full("q0"), ("wf", 1, 2)), (full("q8"),))
+    V(128, cp("ob", al, "a2", S_(0, 128)), (full("a2"),), (full("ob"),))
+    V(128, ts("nob", al, "a2", S_(0, 128), -1.0, None, AO.mult), (full("a2"),), (full("nob"),))
+    V(128, ts("no16", al, "a2", S_(0, 128), -16.0, None, AO.mult), (full("a2"),), (full("no16"),))
+    V(4, ts("lt", al, "i4", al, col("kf", 1), 0.0625, AO.is_ge, AO.mult), (full("i4"), ("kf", 1, 4)), (full("lt"),))
+    V(4, ts("pcon", al, "i44", al, col("kf", 2), None, AO.add), (full("i44"), ("kf", 1, 4)), (full("pcon"),))
+    V(1, ts("kc", S_(0, 1), "kf", S_(1, 2), 128.0, None, AO.add), (("kf", 1, 4),), (("kc", 0, 1),))
+    V(1, ts("kc", S_(1, 2), "kf", S_(1, 2), -64.0, None, AO.add), (("kf", 1, 4),), (("kc", 1, 2),))
+    V(1, ts("tht", S_(0, 1), "thi", al, 4, None, AO.logical_shift_right), (full("thi"),), (("tht", 0, 1),))
+    V(1, ts("tht", S_(1, 2), "thi", al, 15, None, AO.bitwise_and), (full("thi"),), (("tht", 1, 2),))
+    V(2, cp("thf", al, "tht", al), (full("tht"),), (full("thf"),))
+    for k, nm in ((0, "rhi"), (1, "rlo")):
+        V(64, ts(nm, al, "jj", al, col("kf", 3), col("thf", k), AO.is_equal, AO.mult),
+          (full("jj"), ("kf", 1, 4), full("thf")), (full(nm),))
+    for h in (0, 1):
+        for b in range(4):
+            V(16, cp("chh%d" % h, S_(b, 64, 4), "bni", S_(64 * h + 16 * b, 64 * h + 16 * b + 16)),
+              (full("bni"),), (("chh%d" % h, 16 * b, 16 * b + 16),))
+    V(128, cp("win", S_(64, 192), "cni", al), (full("cni"),), (("win", 64, 192),))
+
+    sends = {}
+    for t in range(R):
+        for h in (0, 1):
+            def B(n, h=h):
+                return n + "h%d" % h
+
+            def fb(n, h=h):
+                return full(n + "h%d" % h)
+            PA, PB, PS, PT = B("PA"), B("PB"), B("PS"), B("PT")
+            bank = {k: (k, 0, 512) for k in (PA, PB, PS, PT)}
+            ch, cb = B("ch"), 64 * t
+            chr_ = (ch, cb, cb + 64)
+            if t:
+                add("x%d%d" % (t, h), 0.0, None, (), (chr_,), sem=("ar%d%d" % (t, h), NENG), after=(sends[(t - 1, h)],))
+            bs = 192 if h == 0 else 0
+            wlo, whi = (64, 256) if h == 0 else (0, 192)
+            bslot = ("win", bs, bs + 64)
+
+            def gather(o, src, sc, nc, lo, hi):
+                k = nc // 2
+
+                def ev(g, T):
+                    return g.vector.tensor_copy(T[o][:, 0:16 * k], T["xt"][:, lo:hi].indirect(T[src][:, sc:sc + k]))
+
+                def ea(g, T):
+                    return g.scalar.activation(T[o][:, 16 * k:16 * nc], T["xt"][:, lo:hi].indirect(T[src][:, sc + k:sc + nc]), AF.Copy)
+                rd = (("xt", lo, hi), (src, sc, sc + nc))
+                add("v", 55 + 16 * k * 1.56 * CY, ev, rd, ((o, 0, 16 * k),))
+                add("a", 65 + 16 * (nc - k) * 1.56 * CY, ea, rd, ((o, 16 * k, 16 * nc),))
+
+            def mm(n, P_, os_, lh, ls, rb, rs, st, sp):
+                return (n, lambda T: T[P_][:, os_], lambda T: T[lh][:, ls], lambda T: T[rb][:, rs], st, sp)
+
+            def names(l, n):
+                d, o = B("d%d" % l), B("o%d" % l)
+                k = n // 16
+                P([mm(k, PS, S_(0, k), "pw", S_(15 - r, 143 - r), d, S_(r, n, 16), r == 0, r == 15) for r in range(16)],
+                  (full("pw"), (d, 0, n)), (bank[PS],))
+                ti, tu, tq, tz = [B(x) for x in ("ti", "tu", "tq", "tz")]
+                c = S_(0, k)
+                V(k, cp(ti, c, PS, c), (bank[PS],), (full(ti),))
+                V(k, ts(tu, c, ti, c, 4095, None, AO.bitwise_and), (full(ti),), (full(tu),))
+                V(k, ts(ti, c, tu, c, 592, None, AO.add), (full(tu),), (full(ti),))
+                V(k, tt(tq, c, ti, c, ti, c, AO.mult), (full(ti),), (full(tq),), 2.0)
+                V(k, ts(tz, c, tq, c, 5, 4095, AO.logical_shift_right, AO.bitwise_and), (full(tq),), (full(tz),))
+                V(k, ts(o, c, tz, c, SHIFT[l], None, AO.add), (full(tz),), (full(o),))
+
+            def absop(o, oi, p, n, w):
+                A(n, lambda g, T: g.scalar.activation(T[o][:, oi:oi + n], T[p][:, 0:n], AF.Abs), (bank[p],), w)
+
+            f0, d0 = B("f0"), B("d0")
+            gather(f0, ch, cb, 64, 48, 4144)
+            for s1, pb in ((0, PA), (1, PB)):
+                mms = []
+                for s2 in (0, 1):
+                    for s3 in (0, 1):
+                        q = 4 * s3 + 2 * s2 + s1
+                        for kind in (0, 1):
+                            x = ((s2 * 2 + s3) * 2 + kind) * 64
+                            for z in (0, 1):
+                                rs = S_(64 * (2 * q + z), 64 * (2 * q + z) + 64) if kind == 0 else S_(2 * q + z, 1024, 16)
+                                mms.append(mm(64, pb, S_(x, x + 64), ("idn", "nid")[z], al, f0, rs, z == 0, z == 1))
+                P(mms, (full(f0), full("idn"), full("nid")), (bank[pb],))
+                absop(d0, 512 * s1, pb, 512, ((d0, 512 * s1, 512 * s1 + 512),))
+            V(64, cp("win", S_(bs, bs + 64), ch, S_(cb, cb + 64)), (chr_,), (bslot,))
+            names(0, 1024)
+            for l, n, pb in ((1, 512, PA), (2, 256, PB), (3, 128, PA)):
+                fl, dl = B("f%d" % l), B("d%d" % l)
+                gather(fl, B("o%d" % (l - 1)), 0, n // 8, WINS[l - 1][0], WINS[l - 1][1])
+                P([mm(n, pb, S_(0, n), "idn", al, fl, S_(0, n), True, False),
+                   mm(n, pb, S_(0, n), "nid", al, fl, S_(n, 2 * n), False, True)],
+                  (full(fl), full("idn"), full("nid")), (bank[pb],))
+                absop(dl, 0, pb, n, (full(dl),))
+                names(l, n)
+            w4 = B("w4")
+            gather(w4, B("o3"), 0, 8, WINS[3][0], WINS[3][1])
+            mms = []
+            for b in range(4):
+                mms.append(mm(16, PA, S_(b, 64, 4), "idn", al, w4, S_(16 * b, 16 * b + 16), True, False))
+                mms.append(mm(16, PA, S_(b, 64, 4), "nid", al, w4, S_(64 + b, 128, 4), False, True))
+            P(mms, (full(w4), full("idn"), full("nid")), (bank[PA],))
+            dw = B("dw")
+            absop(dw, 0, PA, 64, (full(dw),))
+            nd = 4 + 4 * h
+            mms = []
+            rd = [full(w4), full("wb8"), full("q8"), full("idn"), full("lt")]
+            if h:
+                mms.append(mm(4, PB, S_(0, 4), "wb8", al, "w4h0", S_(0, 64, 16), True, True))
+                rd.append(full("w4h0"))
+            mms.append(mm(4, PB, S_(nd - 4, nd), "wb8", al, w4, S_(0, 64, 16), True, False))
+            mms.append(mm(4, PB, S_(nd - 4, nd), "idn", al, "lt", al, False, True))
+            for b in range(4):
+                mms.append(mm(1, PB, S_(nd, nd + 1), "q8", S_(3 - b, 131 - b), w4, S_(16 * b, 16 * b + 1), b == 0, b == 3))
+            P(mms, tuple(rd), (bank[PB],))
+            mms = []
+            for b in range(4):
+                mms.append(mm(16, PS, S_(b, 64, 4), "ob", al, w4, S_(16 * b, 16 * b + 16), True, True))
+            for b in range(4):
+                mms.append(mm(16, PS, S_(64 + b, 128, 4), "ob", al, w4, S_(16 * b, 16 * b + 16), True, False))
+                mms.append(mm(16, PS, S_(64 + b, 128, 4), "nob", al, w4, S_(64 + b, 128, 4), False, True))
+            P(mms, (full(w4), full("ob"), full("nob")), (bank[PS],))
+            P([mm(64, PT, S_(0, 64), "no16", al, "rhi", al, True, False),
+               mm(64, PT, S_(0, 64), "nob", al, "rlo", al, False, False)],
+              (full("no16"), full("nob"), full("rhi"), full("rlo")), (bank[PT],))
+            P([mm(64, PT, S_(0, 64), "ob", al, dw, al, False, True)], (full("ob"), full(dw)), (bank[PT],))
+            rr, ff = B("rr"), B("ff")
+            nn = S_(0, nd + 1)
+            V(nd, ts(rr, nn, PB, nn, -0.46875, None, AO.add), (bank[PB],), (full(rr),))
+            V(nd, tt(ff, nn, PB, nn, rr, nn, AO.subtract), (bank[PB], full(rr)), (full(ff),))
+            ds, de, eq, us, t2, s1n, oc = [B(x) for x in ("ds", "de", "eq", "us", "tt", "s1", "oc")]
+            own = col(ff, nd)
+            A(1, lambda g, T, ds=ds, ff=ff, nd=nd, h=h: g.scalar.activation(
+                T[ds][:], T[ff][:, nd:nd + 1], AF.Copy, bias=64.0 * h, scale=128.0), (full(ff),), (full(ds),))
+            A(1, lambda g, T, de=de, ff=ff, nd=nd, h=h: g.scalar.activation(
+                T[de][:], T[ff][:, nd:nd + 1], AF.Identity, bias=T["kc"][:, h:h + 1], scale=-128.0),
+              (full(ff), full("kc")), (full(de),))
+            V(nd, ts(eq, S_(0, nd), ff, S_(0, nd), own, None, AO.is_equal), (full(ff),), (full(eq),))
+            V(nd, lambda g, T, us=us, eq=eq, nd=nd: g.vector.tensor_reduce(T[us][:], T[eq][:, 0:nd], AxisListType.X, AO.max),
+              (full(eq),), (full(us),))
+            V(1, ts(t2, al, us, al, col(de, 0), col(ds, 0), AO.mult, AO.add), (full(us), full(de), full(ds)), (full(t2),))
+            V(1, ts(s1n, al, us, al, 3.0, 1.0, AO.mult, AO.add), (full(us),), (full(s1n),))
+            V(4, ts(oc, al, "pcon", al, col(s1n, 0), col(t2, 0), AO.mult, AO.add), (full("pcon"), full(s1n), full(t2)), (full(oc),))
+            gc = B("gc")
+            add("a", 65 + 100 * CY, lambda g, T, gc=gc, oc=oc, wlo=wlo, whi=whi: g.scalar.activation(
+                T[gc][:], T["win"][:, wlo:whi].indirect(T[oc][:]), AF.Copy), (("win", wlo, whi), full(oc)), (full(gc),))
+            ai, am, a3, qq, mc, mr = [B(x) for x in ("ai", "am", "a3", "qq", "mc", "mr")]
+            V(64, cp(ai, al, PS, S_(0, 64)), (bank[PS],), (full(ai),))
+            A(64, lambda g, T, PS=PS: g.scalar.activation(T[PS][:, 128:192], T[PS][:, 64:128], AF.Relu, scale=8192.0),
+              (bank[PS],), (bank[PS],))
+            cw = S_(128, 192)
+            V(64, ts(am, al, ai, al, 15, None, AO.bitwise_and), (full(ai),), (full(am),))
+            V(64, tt(a3, al, am, al, PS, cw, AO.add), (full(am), bank[PS]), (full(a3),))
+            V(64, tt(mc, al, PT, S_(0, 64), a3, al, AO.is_gt), (bank[PT], full(a3)), (full(mc),))
+            V(64, tt(qq, al, PT, S_(0, 64), am, al, AO.is_gt), (bank[PT], full(am)), (full(qq),))
+            V(64, tt(mr, al, qq, al, PS, cw, AO.min), (full(qq), bank[PS]), (full(mr),))
+            P([mm(4, PA, S_(0, 4), "p16", S_(15 - r, 143 - r), mc, S_(4 * r, 4 * r + 4), r == 0, r == 15) for r in range(16)],
+              (full("p16"), full(mc)), (bank[PA],))
+            ee, me = B("ee"), B("me")
+            V(64, tt(ee, al, gc, al, "win", S_(bs, bs + 64), AO.subtract), (full(gc), bslot), (full(ee),), 2.0)
+            for b in range(4):
+                x = 64 + 16 * b
+                V(16, ts(PT, S_(64 + b, 128, 4), mr, S_(b, 64, 4), col(PA, b), None, AO.not_equal), (full(mr), bank[PA]), ((PT, x, x + 16),))
+            V(64, tt(me, al, PT, S_(64, 128), ee, al, AO.mult), ((PT, 64, 128), full(ee)), (full(me),))
+            if t < R - 1:
+                bn2, co = B("bn2"), B("co")
+                V(64, tt(bn2, al, "win", S_(bs, bs + 64), me, al, AO.add), (bslot, full(me)), (full(bn2),), 2.0)
+                V(64, cp(co, S_(cb, cb + 64), bn2, al), (full(bn2),), ((co, cb, cb + 64),))
+                sends[(t, h)] = add("g", 500.0, ("send", t, h), ((co, cb, cb + 64),), ())
+            else:
+                for b in range(4):
+                    x = 64 * h + 16 * b
+                    V(16, tt("ybt", S_(x, x + 16), "win", S_(bs + b, bs + 64, 4), me, S_(b, 64, 4), AO.add),
+                      (bslot, full(me)), (("ybt", x, x + 16),), 2.0)
+                D("s", "sb%d" % h, lambda T, h=h: T.yb[:, 64 * h:64 * h + 64], lambda T, h=h: T.ybt[:, 64 * h:64 * h + 64],
+                  2000.0, (("ybt", 64 * h, 64 * h + 64),), ())
+            add("v", 50 + 64 * 3.0 * CY, lambda g, T, gc=gc, me=me, oc=oc, wlo=wlo, whi=whi: g.vector.tensor_tensor(
+                T["win"][:, wlo:whi].indirect(T[oc][:]), T[gc][:], T[me][:], AO.subtract),
+                (full(gc), full(me), full(oc)), (("win", wlo, whi),))
+            qs = B("qs")
+            if t == 0:
+                V(64, cp(qs, al, qq, al), (full(qq),), (full(qs),), 0.5)
+            else:
+                V(64, tt(qs, al, qs, al, qq, al, AO.add), (full(qs), full(qq)), (full(qs),), 2.0)
+            if t == R - 1:
+                P([mm(4, PT, S_(0, 4), "p16", S_(15 - r, 143 - r), qs, S_(4 * r, 4 * r + 4), r == 0, r == 15) for r in range(16)],
+                  (full("p16"), full(qs)), (bank[PT],))
+                V(4, cp("yqt", S_(4 * h, 4 * h + 4), PT, S_(0, 4)), (bank[PT],), (("yqt", 4 * h, 4 * h + 4),))
+    D("s", "sq", lambda T: T.yq[:], lambda T: T.yqt[:], 2000.0, (full("yqt"),), ())
+    D("s", "sc", lambda T: T.yc[:], lambda T: T.win[:, 64:192], 2000.0, (("win", 64, 192),), ())
+    return ops
+
+
+def schedule(ops):
+    n = len(ops)
+    succ = [[] for _ in range(n)]
+
+    def lat(j, i):
+        if j in ops[i]["late"]:
+            return HOP
+        if ops[j]["eng"] == ops[i]["eng"] and ops[j]["sem"] is None:
+            return 5.0 if j in ops[i]["waits"] else 0.0
+        return ops[j]["tail"] + 60.0
+    for i in range(n):
+        for j in ops[i]["order"]:
+            succ[j].append(i)
+    pr = [0.0] * n
+    for i in range(n - 1, -1, -1):
+        pr[i] = ops[i]["dur"] + max([ops[i]["tail"]] + [lat(i, k) + pr[k] for k in succ[i]])
+    left = [len(o["order"]) for o in ops]
+    ready = [0.0] * n
+    avail = {}
+    for i in range(n):
+        if not left[i]:
+            avail.setdefault(ops[i]["eng"], []).append(i)
+    free, out, start, end = {}, [], [0.0] * n, [0.0] * n
+    while any(avail.values()):
+        best = None
+        for e, l in avail.items():
+            if not l:
+                continue
+            t = max(free.get(e, 0.0), min(ready[i] for i in l))
+            i = max((x for x in l if ready[x] <= t + 20.0), key=lambda x: (pr[x], -x))
+            t = max(t, ready[i])
+            if best is None or t < best[0]:
+                best = (t, i, e)
+        t, i, e = best
+        avail[e].remove(i)
+        start[i], end[i] = t, t + ops[i]["dur"]
+        free[e] = end[i]
+        out.append(i)
+        for k in succ[i]:
+            ready[k] = max(ready[k], end[i] + lat(i, k))
+            left[k] -= 1
+            if not left[k]:
+                avail.setdefault(ops[k]["eng"], []).append(k)
+    return out, start, end
+
+
+_plan = []
+
+
+def plan():
+    if not _plan:
+        ops = build()
+        order, start, end = schedule(ops)
+        cnt, pos, known, clock, wl = {}, {}, {}, {}, {}
+        for i in order:
+            o = ops[i]
+            e = o["eng"]
+            kn = known.setdefault(e, {})
+            w = []
+            for j in sorted(o["waits"], key=lambda x: -start[x]):
+                s, v = pos[j]
+                if kn.get(s, 0) >= v:
+                    continue
+                w.append((s, v))
+                for s2, v2 in clock[j].items():
+                    if kn.get(s2, 0) < v2:
+                        kn[s2] = v2
+            wl[i] = w
+            if o["sem"] is not None:
+                pos[i] = o["sem"]
+            elif isinstance(o["emit"], tuple):
+                pos[i] = None
+            else:
+                cnt["c" + e] = cnt.get("c" + e, 0) + 1
+                pos[i] = ("c" + e, cnt["c" + e])
+            c = dict(kn)
+            if pos[i]:
+                c[pos[i][0]] = pos[i][1]
+            clock[i] = c
+        _plan.append((ops, order, wl, pos, cnt, start, end))
+    return _plan[0]
+
+
+def relay_of(core, dst, topo):
+    ok = [c for c in topo.cores_of(core) if c != core and topo.may_write(c, dst)]
+    near = [c for c in ok if topo.die(c) == topo.die(core)]
+    return (near or ok)[0]
+
+
+def mask_of(src, dst, topo):
+    return sum(1 << e for e in topo.engines(src, dst)[:NENG])
+
+
+def rank_program(g, core, T, topo):
+    ops, order, wl, pos, cnt, start, end = plan()
+    pieces = [ops[i]["emit"][1:] for i in order if isinstance(ops[i]["emit"], tuple)]
+    rank = T.rank_of(core)
+    if rank is None:
+        for q in range(N):
+            src, dst = T.cores[q], T.cores[(q + H) % N]
+            if relay_of(src, dst, topo) != core:
+                continue
+            rid, pid = topo.addr(dst, core)
+            for t, h in pieces:
+                g.wait_ge(T.sem["rl%d%d" % (t + 1, h)], NENG)
+                tile = T["chh%d" % h][:, 64 * (t + 1):64 * (t + 2)]
+                g.remote_dma(tile, tile, T.sem["ar%d%d" % (t + 1, h)], T.sem.snd, pid, rid, mask_of(core, dst, topo))
+            g.wait_ge(T.sem.snd, NENG * len(pieces))
+        return
+    nxt = T.cores[(rank + H) % N]
+    rel = relay_of(core, nxt, topo)
+    rid, pid = topo.addr(rel, core)
+    queue = {"v": g.vector, "a": g.scalar, "p": g.tensor, "g": g, "s": g.sync}
+    for i in order:
+        o = ops[i]
+        if o["emit"] is None:
+            continue
+        q = queue[o["eng"]]
+        for s, v in wl[i]:
+            q.wait_ge(T.sem[s], v)
+        if isinstance(o["emit"], tuple):
+            t, h = o["emit"][1:]
+            g.remote_dma(T["chh%d" % h][:, 64 * (t + 1):64 * (t + 2)], T["coh%d" % h][:, 64 * t:64 * (t + 1)],
+                         T.sem["rl%d%d" % (t + 1, h)], T.sem.snd, pid, rid, mask_of(core, rel, topo))
+        else:
+            o["emit"](g, T).then_inc(T.sem[pos[i][0]], 16 if o["sem"] else 1)
+    for s in sorted(cnt):
+        g.wait_ge(T.sem[s], cnt[s])
+    for d in DMAS:
+        g.wait_ge(T.sem["m_" + d], 16)
+    for t in range(1, R):
+        for h in (0, 1):
+            g.wait_ge(T.sem["ar%d%d" % (t, h)], NENG)
+    g.wait_ge(T.sem.snd, NENG * len(pieces))

@@ -39,18 +39,23 @@ for _h in (0, 1):
     for _n in ("PA", "PB", "PS", "PT"):
         SCRATCH[_n + "h%d" % _h] = ("psum", [128, 512], "float32")
 
-DMAS = ["lw", "lt", "lb", "lc", "lx", "le", "lf", "ll", "sb0", "sb1", "sc", "sq"]
+DMAS = ["lw", "lt", "lb", "lc", "lx", "le", "lf", "ll", "sb0", "sq", "sb1", "sc"]
 SEMAPHORES = ["cv", "ca", "cp", "cg", "snd"] + ["m_" + d for d in DMAS] + \
              ["ar%d%d" % (t, h) for t in range(1, R) for h in (0, 1)] + ["rl%d%d" % (t, h) for t in range(1, R) for h in (0, 1)]
 
 NENG = 8
-HOP = 5000.0
+HOP, SAME, WAKE, SECOND = 6500.0, 40.0, 60.0, 800.0
 CY = 0.95
 AF, AO = ActivationFunctionType, AluOpType
+G0 = (("v", 0, 16), ("a", 16, 16), ("v", 32, 16), ("v", 48, 16))
+G1 = (("a", 0, 16), ("v", 16, 16), ("a", 32, 16), ("v", 48, 16))
+G2 = (("a", 0, 16), ("v", 16, 16))
+G3 = (("a", 0, 8), ("v", 8, 8))
+G4 = (("a", 0, 8),)
 
 
 def build():
-    ops, track = [], {}
+    ops, track, cur = [], {}, [0]
 
     def add(eng, dur, emit, R_=(), W_=(), tail=0.0, sem=None, after=()):
         i = len(ops)
@@ -74,7 +79,8 @@ def build():
                 waits.add(j)
         for j in after:
             order.add(j)
-        ops.append({"eng": eng, "dur": dur, "emit": emit, "order": order, "waits": waits, "tail": tail, "sem": sem, "late": set(after)})
+        ops.append({"eng": eng, "dur": dur, "emit": emit, "order": order, "waits": waits, "tail": tail, "sem": sem,
+                    "late": set(after), "h": cur[0]})
         for (b, lo, hi), wr in [(x, False) for x in R_] + [(x, True) for x in W_]:
             l = track.setdefault(b, [])
             if wr:
@@ -130,12 +136,12 @@ def build():
     def col(b, c):
         return lambda T: T[b][:, c:c + 1]
 
-    D("a", "lw", lambda T: T.wti[:], lambda T: T.wt[:], 2000.0, (), (full("wti"),))
     D("a", "lb", lambda T: T.bni[:], lambda T: T.bn[:], 2200.0, (), (full("bni"),))
     D("s", "lx", lambda T: T.xt[:, PADL:PADL + 4096], lambda T: T.xf[:], 7500.0, (), (("xt", 48, 4144),))
-    D("a", "lt", lambda T: T.thi[:], lambda T: T.th[:], 2200.0, (), (full("thi"),))
-    D("a", "lc", lambda T: T.cni[:], lambda T: T.cn[:], 2500.0, (), (full("cni"),))
+    D("a", "lw", lambda T: T.wti[:], lambda T: T.wt[:], 2000.0, (), (full("wti"),))
     D("s", "le", lambda T: T.xt[:, 4144:5584], lambda T: T.xf[:, 0:1440], 9500.0, (), (("xt", 4144, 5584),))
+    D("s", "lt", lambda T: T.thi[:], lambda T: T.th[:], 9600.0, (), (full("thi"),))
+    D("s", "lc", lambda T: T.cni[:], lambda T: T.cn[:], 9700.0, (), (full("cni"),))
     D("s", "lf", lambda T: T.xt[:, 5584:6784], lambda T: T.xf[:, 1440:2640], 11500.0, (), (("xt", 5584, 6784),))
     D("s", "ll", lambda T: T.xt[:, 0:48], lambda T: T.xf[:, 4048:4096], 12000.0, (), (("xt", 0, 48),))
     V(144, lambda g, T: g.vector.memset(T.ones[:], 1.0), (), (full("ones"),))
@@ -187,11 +193,10 @@ def build():
     sends = {}
     for t in range(R):
         for h in (0, 1):
+            cur[0] = h
+
             def B(n, h=h):
                 return n + "h%d" % h
-
-            def fb(n, h=h):
-                return full(n + "h%d" % h)
             PA, PB, PS, PT = B("PA"), B("PB"), B("PS"), B("PT")
             bank = {k: (k, 0, 512) for k in (PA, PB, PS, PT)}
             ch, cb = B("ch"), 64 * t
@@ -202,17 +207,21 @@ def build():
             wlo, whi = (64, 256) if h == 0 else (0, 192)
             bslot = ("win", bs, bs + 64)
 
-            def gather(o, src, sc, nc, lo, hi):
-                k = nc // 2
+            def gather(o, src, sc, sn, parts, win):
+                lo, hi = win
 
-                def ev(g, T):
-                    return g.vector.tensor_copy(T[o][:, 0:16 * k], T["xt"][:, lo:hi].indirect(T[src][:, sc:sc + k]))
+                def part(e, c0, nc):
+                    def ev(g, T):
+                        return g.vector.tensor_copy(T[o][:, 16 * c0:16 * (c0 + nc)],
+                                                    T["xt"][:, lo:hi].indirect(T[src][:, sc + c0:sc + c0 + nc]))
 
-                def ea(g, T):
-                    return g.scalar.activation(T[o][:, 16 * k:16 * nc], T["xt"][:, lo:hi].indirect(T[src][:, sc + k:sc + nc]), AF.Copy)
-                rd = (("xt", lo, hi), (src, sc, sc + nc))
-                add("v", 55 + 16 * k * 1.56 * CY, ev, rd, ((o, 0, 16 * k),))
-                add("a", 65 + 16 * (nc - k) * 1.56 * CY, ea, rd, ((o, 16 * k, 16 * nc),))
+                    def ea(g, T):
+                        return g.scalar.activation(T[o][:, 16 * c0:16 * (c0 + nc)],
+                                                   T["xt"][:, lo:hi].indirect(T[src][:, sc + c0:sc + c0 + nc]), AF.Copy)
+                    add(e, (55 if e == "v" else 65) + 16 * nc * 1.56 * CY, ev if e == "v" else ea,
+                        (("xt", lo, hi), (src, sc, sc + sn)), ((o, 16 * c0, 16 * (c0 + nc)),))
+                for p in parts:
+                    part(*p)
 
             def mm(n, P_, os_, lh, ls, rb, rs, st, sp):
                 return (n, lambda T: T[P_][:, os_], lambda T: T[lh][:, ls], lambda T: T[rb][:, rs], st, sp)
@@ -231,42 +240,59 @@ def build():
                 V(k, ts(tz, c, tq, c, 5, 4095, AO.logical_shift_right, AO.bitwise_and), (full(tq),), (full(tz),))
                 V(k, ts(o, c, tz, c, SHIFT[l], None, AO.add), (full(tz),), (full(o),))
 
-            def absop(o, oi, p, n, w):
-                A(n, lambda g, T: g.scalar.activation(T[o][:, oi:oi + n], T[p][:, 0:n], AF.Abs), (bank[p],), w)
+            def absop(o, oi, p, pi, n):
+                A(n, lambda g, T: g.scalar.activation(T[o][:, oi:oi + n], T[p][:, pi:pi + n], AF.Abs), (bank[p],), ((o, oi, oi + n),))
 
+            def diff(n, p, x, f, one, two):
+                return [mm(n, p, S_(x, x + n), "idn", al, f, one, True, False), mm(n, p, S_(x, x + n), "nid", al, f, two, False, True)]
+            eye = (full("idn"), full("nid"))
             f0, d0 = B("f0"), B("d0")
-            gather(f0, ch, cb, 64, 48, 4144)
-            for s1, pb in ((0, PA), (1, PB)):
+            gather(f0, ch, cb, 64, G0, (48, 4144))
+            for k in range(4):
+                pb, y = (PA, PB)[k % 2], 256 * k
                 mms = []
-                for s2 in (0, 1):
-                    for s3 in (0, 1):
-                        q = 4 * s3 + 2 * s2 + s1
-                        for kind in (0, 1):
-                            x = ((s2 * 2 + s3) * 2 + kind) * 64
-                            for z in (0, 1):
-                                rs = S_(64 * (2 * q + z), 64 * (2 * q + z) + 64) if kind == 0 else S_(2 * q + z, 1024, 16)
-                                mms.append(mm(64, pb, S_(x, x + 64), ("idn", "nid")[z], al, f0, rs, z == 0, z == 1))
-                P(mms, (full(f0), full("idn"), full("nid")), (bank[pb],))
-                absop(d0, 512 * s1, pb, 512, ((d0, 512 * s1, 512 * s1 + 512),))
+                for z in (0, 1):
+                    mms += diff(64, pb, 64 * z, f0, S_(y + 128 * z, y + 128 * z + 64), S_(y + 128 * z + 64, y + 128 * z + 128))
+                mms += diff(128, pb, 128, f0, S_(y, y + 256, 2), S_(y + 1, y + 256, 2))
+                P(mms, ((f0, y, y + 256),) + eye, (bank[pb],))
+                absop(d0, y, pb, 0, 256)
             V(64, cp("win", S_(bs, bs + 64), ch, S_(cb, cb + 64)), (chr_,), (bslot,))
             names(0, 1024)
-            for l, n, pb in ((1, 512, PA), (2, 256, PB), (3, 128, PA)):
-                fl, dl = B("f%d" % l), B("d%d" % l)
-                gather(fl, B("o%d" % (l - 1)), 0, n // 8, WINS[l - 1][0], WINS[l - 1][1])
-                P([mm(n, pb, S_(0, n), "idn", al, fl, S_(0, n), True, False),
-                   mm(n, pb, S_(0, n), "nid", al, fl, S_(n, 2 * n), False, True)],
-                  (full(fl), full("idn"), full("nid")), (bank[pb],))
-                absop(dl, 0, pb, n, (full(dl),))
-                names(l, n)
+            f1, d1 = B("f1"), B("d1")
+            gather(f1, B("o0"), 0, 64, G1, WINS[0])
+            for k in (0, 1):
+                pb, mms = (PA, PB)[k], []
+                for z in (0, 1):
+                    y = 512 * k + 256 * z
+                    mms += diff(64, pb, 64 * z, f1, S_(y, y + 64), S_(y + 64, y + 128))
+                    mms += diff(64, pb, 128 + 64 * z, f1, S_(y + 128, y + 256, 2), S_(y + 129, y + 256, 2))
+                P(mms, ((f1, 512 * k, 512 * k + 512),) + eye, (bank[pb],))
+                absop(d1, 256 * k, pb, 0, 256)
+            names(1, 512)
+            f2, d2 = B("f2"), B("d2")
+            gather(f2, B("o1"), 0, 32, G2, WINS[1])
+            for k in (0, 1):
+                y = 256 * k
+                P(diff(64, PA, 64 * k, f2, S_(y, y + 64), S_(y + 64, y + 128)) +
+                  diff(64, PA, 128 + 64 * k, f2, S_(y + 128, y + 256, 2), S_(y + 129, y + 256, 2)),
+                  ((f2, y, y + 256),) + eye, ((PA, 256 * k, 256 * k + 256),))
+            absop(d2, 0, PA, 0, 256)
+            names(2, 256)
+            f3, d3 = B("f3"), B("d3")
+            gather(f3, B("o2"), 0, 16, G3, WINS[2])
+            P(diff(64, PB, 0, f3, S_(0, 64), S_(64, 128)), ((f3, 0, 128),) + eye, ((PB, 0, 64),))
+            P(diff(64, PB, 64, f3, S_(128, 256, 2), S_(129, 256, 2)), ((f3, 128, 256),) + eye, ((PB, 64, 128),))
+            absop(d3, 0, PB, 0, 128)
+            names(3, 128)
             w4 = B("w4")
-            gather(w4, B("o3"), 0, 8, WINS[3][0], WINS[3][1])
+            gather(w4, B("o3"), 0, 8, G4, WINS[3])
             mms = []
             for b in range(4):
                 mms.append(mm(16, PA, S_(b, 64, 4), "idn", al, w4, S_(16 * b, 16 * b + 16), True, False))
                 mms.append(mm(16, PA, S_(b, 64, 4), "nid", al, w4, S_(64 + b, 128, 4), False, True))
-            P(mms, (full(w4), full("idn"), full("nid")), (bank[PA],))
+            P(mms, (full(w4),) + eye, (bank[PA],))
             dw = B("dw")
-            absop(dw, 0, PA, 64, (full(dw),))
+            absop(dw, 0, PA, 0, 64)
             nd = 4 + 4 * h
             mms = []
             rd = [full(w4), full("wb8"), full("q8"), full("idn"), full("lt")]
@@ -351,6 +377,7 @@ def build():
                 P([mm(4, PT, S_(0, 4), "p16", S_(15 - r, 143 - r), qs, S_(4 * r, 4 * r + 4), r == 0, r == 15) for r in range(16)],
                   (full("p16"), full(qs)), (bank[PT],))
                 V(4, cp("yqt", S_(4 * h, 4 * h + 4), PT, S_(0, 4)), (bank[PT],), (("yqt", 4 * h, 4 * h + 4),))
+    cur[0] = 0
     D("s", "sq", lambda T: T.yq[:], lambda T: T.yqt[:], 2000.0, (full("yqt"),), ())
     D("s", "sc", lambda T: T.yc[:], lambda T: T.win[:, 64:192], 2000.0, (("win", 64, 192),), ())
     return ops
@@ -364,14 +391,15 @@ def schedule(ops):
         if j in ops[i]["late"]:
             return HOP
         if ops[j]["eng"] == ops[i]["eng"] and ops[j]["sem"] is None:
-            return 5.0 if j in ops[i]["waits"] else 0.0
-        return ops[j]["tail"] + 60.0
+            return SAME if j in ops[i]["waits"] else 0.0
+        return ops[j]["tail"] + WAKE
     for i in range(n):
         for j in ops[i]["order"]:
             succ[j].append(i)
     pr = [0.0] * n
     for i in range(n - 1, -1, -1):
         pr[i] = ops[i]["dur"] + max([ops[i]["tail"]] + [lat(i, k) + pr[k] for k in succ[i]])
+    key = [pr[i] - SECOND * ops[i]["h"] for i in range(n)]
     left = [len(o["order"]) for o in ops]
     ready = [0.0] * n
     avail = {}
@@ -385,7 +413,7 @@ def schedule(ops):
             if not l:
                 continue
             t = max(free.get(e, 0.0), min(ready[i] for i in l))
-            i = max((x for x in l if ready[x] <= t + 20.0), key=lambda x: (pr[x], -x))
+            i = max((x for x in l if ready[x] <= t + 20.0), key=lambda x: (key[x], -x))
             t = max(t, ready[i])
             if best is None or t < best[0]:
                 best = (t, i, e)
@@ -482,11 +510,13 @@ def rank_program(g, core, T, topo):
                          T.sem["rl%d%d" % (t + 1, h)], T.sem.snd, pid, rid, mask_of(core, rel, topo))
         else:
             o["emit"](g, T).then_inc(T.sem[pos[i][0]], 16 if o["sem"] else 1)
-    for s in sorted(cnt):
-        g.wait_ge(T.sem[s], cnt[s])
-    for d in DMAS:
-        g.wait_ge(T.sem["m_" + d], 16)
+    g.wait_ge(T.sem.snd, NENG * len(pieces))
     for t in range(1, R):
         for h in (0, 1):
             g.wait_ge(T.sem["ar%d%d" % (t, h)], NENG)
-    g.wait_ge(T.sem.snd, NENG * len(pieces))
+    for d in DMAS[:8]:
+        g.wait_ge(T.sem["m_" + d], 16)
+    for s in ("cg", "cp", "ca", "cv"):
+        g.wait_ge(T.sem[s], cnt[s])
+    for d in DMAS[8:]:
+        g.wait_ge(T.sem["m_" + d], 16)

from concourse.mybir import dt, AluOpType, AxisListType, ActivationFunctionType

R, H, N = 4, 5, 8
KAP = (101, 1303, 2717, 3911)
PADL = 48
SHIFT = (1437, 2639, 5, 1151)
WINS = ((48, 5584), (48, 6784), (0, 4112), (48, 5296))

SCRATCH = {"xt": ("sbuf", [128, 6784], "bfloat16")}


def _sb(name, cols, d):
    SCRATCH[name] = ("sbuf", [128, cols], d)


for _n, _c, _d in (("bni", 128, "int32"), ("cni", 128, "int32"), ("wti", 1, "int32"), ("thi", 1, "int32"),
                   ("ones", 144, "float32"), ("a1", 144, "float32"), ("a2", 144, "float32"), ("p0", 144, "float32"),
                   ("q0", 144, "float32"), ("idf", 128, "float32"), ("ki", 4, "int32"), ("kf", 4, "float32"),
                   ("wf", 2, "float32"), ("tht", 2, "int32"), ("thf", 2, "float32"), ("i4", 4, "float32"),
                   ("i44", 4, "float32"), ("jj", 64, "float32"), ("pcon", 4, "float32"), ("kc", 2, "float32"),
                   ("pw", 144, "bfloat16"), ("p16", 144, "bfloat16"), ("wb8", 128, "bfloat16"), ("q8", 144, "bfloat16"),
                   ("idn", 128, "bfloat16"), ("nid", 128, "bfloat16"), ("ob", 128, "bfloat16"), ("nob", 128, "bfloat16"),
                   ("no16", 128, "bfloat16"), ("lt", 4, "bfloat16"), ("rhi", 64, "bfloat16"), ("rlo", 64, "bfloat16"),
                   ("win", 256, "float32"), ("ybt", 128, "float32"), ("yqt", 8, "float32")):
    _sb(_n, _c, _d)
for _h in (0, 1):
    for _n, _c, _d in (("f0", 1024, "bfloat16"), ("f1", 1024, "bfloat16"), ("f2", 512, "bfloat16"), ("f3", 256, "bfloat16"),
                       ("w4", 128, "bfloat16"), ("d0", 1024, "bfloat16"), ("d1", 512, "bfloat16"), ("d2", 256, "bfloat16"),
                       ("d3", 128, "bfloat16"), ("dw", 64, "bfloat16"), ("ti", 64, "int32"), ("tu", 64, "int32"),
                       ("tq", 64, "int32"), ("tz", 64, "int32"), ("o0", 64, "uint16"),
                       ("o1", 32, "uint16"), ("o2", 16, "uint16"), ("o3", 8, "uint16"), ("rr", 12, "int32"),
                       ("ff", 12, "float32"), ("ds", 1, "float32"), ("de", 1, "float32"), ("eq", 8, "float32"),
                       ("us", 1, "float32"), ("tt", 1, "float32"), ("s1", 1, "float32"), ("oc", 4, "uint16"),
                       ("gc", 64, "float32"), ("ai", 64, "int32"), ("am", 64, "int32"), ("a3", 64, "float32"),
                       ("qq", 64, "bfloat16"), ("mc", 64, "bfloat16"), ("mr", 64, "bfloat16"),
                       ("ee", 64, "float32"), ("me", 64, "float32"), ("bn2", 64, "float32"), ("qs", 64, "bfloat16"),
                       ("ch", 64 * R, "uint16"), ("co", 64 * R, "uint16")):
        _sb(_n + "h%d" % _h, _c, _d)
    for _n in ("PA", "PB", "PS", "PT"):
        SCRATCH[_n + "h%d" % _h] = ("psum", [128, 512], "float32")

DMAS = ["lw", "lt", "lb", "lc", "lx", "le", "lf", "ll", "sb0", "sq", "sb1", "sc"]
SEMAPHORES = ["cv", "ca", "cp", "cg", "snd"] + ["m_" + d for d in DMAS] + \
             ["ar%d%d" % (t, h) for t in range(1, R) for h in (0, 1)] + ["rl%d%d" % (t, h) for t in range(1, R) for h in (0, 1)]

NENG = 8
HOP, SAME, WAKE, SECOND = 6500.0, 40.0, 60.0, 800.0
CY = 0.95
AF, AO = ActivationFunctionType, AluOpType
G0 = (("v", 0, 16), ("a", 16, 16), ("v", 32, 16), ("v", 48, 16))
G1 = (("a", 0, 16), ("v", 16, 16), ("a", 32, 16), ("v", 48, 16))
G2 = (("a", 0, 16), ("v", 16, 16))
G3 = (("a", 0, 8), ("v", 8, 8))
G4 = (("a", 0, 8),)


def build():
    ops, track, cur = [], {}, [0]

    def add(eng, dur, emit, R_=(), W_=(), tail=0.0, sem=None, after=()):
        i = len(ops)
        order, waits = set(), set()
        for (b, lo, hi), wr in [(x, False) for x in R_] + [(x, True) for x in W_]:
            ps = b[0] == "P"
            for (lo2, hi2, j, wr2) in track.get(b, ()):
                if j == i:
                    continue
                e2 = ops[j]["eng"]
                clash = lo < hi2 and lo2 < hi
                if ps and e2 != eng:
                    clash = True
                elif not (wr or wr2):
                    clash = False
                if not clash:
                    continue
                order.add(j)
                if e2 == eng == "p":
                    continue
                waits.add(j)
        for j in after:
            order.add(j)
        ops.append({"eng": eng, "dur": dur, "emit": emit, "order": order, "waits": waits, "tail": tail, "sem": sem,
                    "late": set(after), "h": cur[0]})
        for (b, lo, hi), wr in [(x, False) for x in R_] + [(x, True) for x in W_]:
            l = track.setdefault(b, [])
            if wr:
                l[:] = [e for e in l if e[2] == i or not (lo <= e[0] and e[1] <= hi)]
            l.append((lo, hi, i, wr))
        return i

    def V(n, emit, R_, W_, f=1.0):
        return add("v", 10 + max(64, n * f) * CY, emit, R_, W_)

    def A(n, emit, R_, W_):
        return add("a", 20 + max(64, n) * CY, emit, R_, W_)

    def G(n, emit, R_, W_):
        return add("g", 150 + 2 * n * CY, emit, R_, W_)

    def P(mms, R_, W_):
        dur = 10 + sum(max(64, m[0]) * 0.42 for m in mms)

        def emit(g, T):
            for m in mms:
                last = g.tensor.matmul(m[1](T), m[2](T), m[3](T), m[4], m[5])
            return last
        return add("p", dur, emit, R_, W_)

    def D(q, name, out, in_, dur, R_, W_):
        def emit(g, T):
            return (g.sync if q == "s" else g.scalar).dma_start(out(T), in_(T))
        return add(q, 60.0, emit, R_, W_, tail=dur, sem=("m_" + name, 16))

    def full(b):
        return (b, 0, SCRATCH[b][1][1])

    def val(x, T):
        return x if x is None or isinstance(x, (int, float)) else x(T)

    def ts(o, oi, a, ai, s1, s2, op0, op1=None):
        def emit(g, T):
            if op1 is None:
                return g.vector.tensor_scalar(T[o][:, oi], T[a][:, ai], val(s1, T), None, op0=op0)
            return g.vector.tensor_scalar(T[o][:, oi], T[a][:, ai], val(s1, T), val(s2, T), op0=op0, op1=op1)
        return emit

    def cp(o, oi, a, ai):
        return lambda g, T: g.vector.tensor_copy(T[o][:, oi], T[a][:, ai])

    def tt(o, oi, a, ai, b, bi, op):
        return lambda g, T: g.vector.tensor_tensor(T[o][:, oi], T[a][:, ai], T[b][:, bi], op)

    S_ = slice
    al = S_(None)

    def col(b, c):
        return lambda T: T[b][:, c:c + 1]

    D("a", "lb", lambda T: T.bni[:], lambda T: T.bn[:], 2200.0, (), (full("bni"),))
    D("s", "lx", lambda T: T.xt[:, PADL:PADL + 4096], lambda T: T.xf[:], 7500.0, (), (("xt", 48, 4144),))
    D("a", "lw", lambda T: T.wti[:], lambda T: T.wt[:], 2000.0, (), (full("wti"),))
    D("s", "le", lambda T: T.xt[:, 4144:5584], lambda T: T.xf[:, 0:1440], 9500.0, (), (("xt", 4144, 5584),))
    D("s", "lt", lambda T: T.thi[:], lambda T: T.th[:], 9600.0, (), (full("thi"),))
    D("s", "lc", lambda T: T.cni[:], lambda T: T.cn[:], 9700.0, (), (full("cni"),))
    D("s", "lf", lambda T: T.xt[:, 5584:6784], lambda T: T.xf[:, 1440:2640], 11500.0, (), (("xt", 5584, 6784),))
    D("s", "ll", lambda T: T.xt[:, 0:48], lambda T: T.xf[:, 4048:4096], 12000.0, (), (("xt", 0, 48),))
    V(144, lambda g, T: g.vector.memset(T.ones[:], 1.0), (), (full("ones"),))
    G(1, lambda g, T: g.iota(T.ki[:, 0:1], [[1, 1]], 0, 1), (), (("ki", 0, 1),))
    G(128, lambda g, T: g.affine_select(T.idf[:], T.ones[:, 0:128], [[-1, 128]], AO.is_equal, 0.0, 0, 1),
      (full("ones"),), (full("idf"),))
    G(144, lambda g, T: g.affine_select(T.a1[:], T.ones[:], [[-16, 9], [0, 16]], AO.is_ge, 0.0, 0, 1),
      (full("ones"),), (full("a1"),))
    G(144, lambda g, T: g.affine_select(T.a2[:], T.a1[:], [[16, 9], [0, 16]], AO.is_ge, 0.0, 15, -1),
      (full("a1"),), (full("a2"),))
    G(144, lambda g, T: g.affine_select(T.p0[:], T.a2[:], [[0, 9], [1, 16]], AO.is_equal, 0.0, -15, 0),
      (full("a2"),), (full("p0"),))
    G(144, lambda g, T: g.affine_select(T.q0[:], T.a2[:], [[0, 36], [1, 4]], AO.is_equal, 0.0, -3, 0),
      (full("a2"),), (full("q0"),))
    G(4, lambda g, T: g.iota(T.i4[:], [[1, 4]], 0, 0, allow_small_or_imprecise_dtypes=True), (), (full("i4"),))
    G(4, lambda g, T: g.iota(T.i44[:], [[4, 4]], 0, 0, allow_small_or_imprecise_dtypes=True), (), (full("i44"),))
    G(64, lambda g, T: g.iota(T.jj[:], [[1, 16], [0, 4]], 0, 0, allow_small_or_imprecise_dtypes=True), (), (full("jj"),))
    V(1, cp("wf", S_(0, 1), "wti", al), (full("wti"),), (("wf", 0, 1),))
    V(1, ts("wf", S_(1, 2), "wti", al, 0.125, None, AO.mult), (full("wti"),), (("wf", 1, 2),))
    V(1, ts("ki", S_(1, 2), "ki", S_(0, 1), 3, None, AO.bitwise_and), (("ki", 0, 1),), (("ki", 1, 2),))
    V(1, ts("ki", S_(2, 3), "ki", S_(0, 1), 2, 3, AO.logical_shift_right, AO.bitwise_and), (("ki", 0, 1),), (("ki", 2, 3),))
    V(1, ts("ki", S_(3, 4), "ki", S_(0, 1), 15, None, AO.bitwise_and), (("ki", 0, 1),), (("ki", 3, 4),))
    V(3, cp("kf", S_(1, 4), "ki", S_(1, 4)), (("ki", 1, 4),), (("kf", 1, 4),))
    V(128, cp("idn", al, "idf", al), (full("idf"),), (full("idn"),))
    V(128, ts("nid", al, "idf", al, -1.0, None, AO.mult), (full("idf"),), (full("nid"),))
    V(144, ts("pw", al, "p0", al, col("wf", 0), None, AO.mult), (full("p0"), ("wf", 0, 1)), (full("pw"),))
    V(144, ts("p16", al, "p0", al, 0.0625, None, AO.mult), (full("p0"),), (full("p16"),))
    V(128, ts("wb8", al, "a2", S_(0, 128), col("wf", 1), None, AO.mult), (full("a2"), ("wf", 1, 2)), (full("wb8"),))
    V(144, ts("q8", al, "q0", al, col("wf", 1), None, AO.mult), (full("q0"), ("wf", 1, 2)), (full("q8"),))
    V(128, cp("ob", al, "a2", S_(0, 128)), (full("a2"),), (full("ob"),))
    V(128, ts("nob", al, "a2", S_(0, 128), -1.0, None, AO.mult), (full("a2"),), (full("nob"),))
    V(128, ts("no16", al, "a2", S_(0, 128), -16.0, None, AO.mult), (full("a2"),), (full("no16"),))
    V(4, ts("lt", al, "i4", al, col("kf", 1), 0.0625, AO.is_ge, AO.mult), (full("i4"), ("kf", 1, 4)), (full("lt"),))
    V(4, ts("pcon", al, "i44", al, col("kf", 2), None, AO.add), (full("i44"), ("kf", 1, 4)), (full("pcon"),))
    V(1, ts("kc", S_(0, 1), "kf", S_(1, 2), 128.0, None, AO.add), (("kf", 1, 4),), (("kc", 0, 1),))
    V(1, ts("kc", S_(1, 2), "kf", S_(1, 2), -64.0, None, AO.add), (("kf", 1, 4),), (("kc", 1, 2),))
    V(1, ts("tht", S_(0, 1), "thi", al, 4, None, AO.logical_shift_right), (full("thi"),), (("tht", 0, 1),))
    V(1, ts("tht", S_(1, 2), "thi", al, 15, None, AO.bitwise_and), (full("thi"),), (("tht", 1, 2),))
    V(2, cp("thf", al, "tht", al), (full("tht"),), (full("thf"),))
    for k, nm in ((0, "rhi"), (1, "rlo")):
        V(64, ts(nm, al, "jj", al, col("kf", 3), col("thf", k), AO.is_equal, AO.mult),
          (full("jj"), ("kf", 1, 4), full("thf")), (full(nm),))
    for h in (0, 1):
        for b in range(4):
            V(16, cp("chh%d" % h, S_(b, 64, 4), "bni", S_(64 * h + 16 * b, 64 * h + 16 * b + 16)),
              (full("bni"),), (("chh%d" % h, 16 * b, 16 * b + 16),))
    V(128, cp("win", S_(64, 192), "cni", al), (full("cni"),), (("win", 64, 192),))

    sends = {}
    for t in range(R):
        for h in (0, 1):
            cur[0] = h

            def B(n, h=h):
                return n + "h%d" % h
            PA, PB, PS, PT = B("PA"), B("PB"), B("PS"), B("PT")
            bank = {k: (k, 0, 512) for k in (PA, PB, PS, PT)}
            ch, cb = B("ch"), 64 * t
            chr_ = (ch, cb, cb + 64)
            if t:
                add("x%d%d" % (t, h), 0.0, None, (), (chr_,), sem=("ar%d%d" % (t, h), NENG), after=(sends[(t - 1, h)],))
            bs = 192 if h == 0 else 0
            wlo, whi = (64, 256) if h == 0 else (0, 192)
            bslot = ("win", bs, bs + 64)

            def gather(o, src, sc, sn, parts, win):
                lo, hi = win

                def part(e, c0, nc):
                    def ev(g, T):
                        return g.vector.tensor_copy(T[o][:, 16 * c0:16 * (c0 + nc)],
                                                    T["xt"][:, lo:hi].indirect(T[src][:, sc + c0:sc + c0 + nc]))

                    def ea(g, T):
                        return g.scalar.activation(T[o][:, 16 * c0:16 * (c0 + nc)],
                                                   T["xt"][:, lo:hi].indirect(T[src][:, sc + c0:sc + c0 + nc]), AF.Copy)
                    add(e, (55 if e == "v" else 65) + 16 * nc * 1.56 * CY, ev if e == "v" else ea,
                        (("xt", lo, hi), (src, sc, sc + sn)), ((o, 16 * c0, 16 * (c0 + nc)),))
                for p in parts:
                    part(*p)

            def mm(n, P_, os_, lh, ls, rb, rs, st, sp):
                return (n, lambda T: T[P_][:, os_], lambda T: T[lh][:, ls], lambda T: T[rb][:, rs], st, sp)

            def names(l, n):
                d, o = B("d%d" % l), B("o%d" % l)
                k = n // 16
                P([mm(k, PS, S_(0, k), "pw", S_(15 - r, 143 - r), d, S_(r, n, 16), r == 0, r == 15) for r in range(16)],
                  (full("pw"), (d, 0, n)), (bank[PS],))
                ti, tu, tq, tz = [B(x) for x in ("ti", "tu", "tq", "tz")]
                c = S_(0, k)
                V(k, cp(ti, c, PS, c), (bank[PS],), (full(ti),))
                V(k, ts(tu, c, ti, c, 4095, None, AO.bitwise_and), (full(ti),), (full(tu),))
                V(k, ts(ti, c, tu, c, 592, None, AO.add), (full(tu),), (full(ti),))
                V(k, tt(tq, c, ti, c, ti, c, AO.mult), (full(ti),), (full(tq),), 2.0)
                V(k, ts(tz, c, tq, c, 5, 4095, AO.logical_shift_right, AO.bitwise_and), (full(tq),), (full(tz),))
                V(k, ts(o, c, tz, c, SHIFT[l], None, AO.add), (full(tz),), (full(o),))

            def absop(o, oi, p, pi, n):
                A(n, lambda g, T: g.scalar.activation(T[o][:, oi:oi + n], T[p][:, pi:pi + n], AF.Abs), (bank[p],), ((o, oi, oi + n),))

            def diff(n, p, x, f, one, two):
                return [mm(n, p, S_(x, x + n), "idn", al, f, one, True, False), mm(n, p, S_(x, x + n), "nid", al, f, two, False, True)]
            eye = (full("idn"), full("nid"))
            f0, d0 = B("f0"), B("d0")
            gather(f0, ch, cb, 64, G0, (48, 4144))
            for k in range(4):
                pb, y = (PA, PB)[k % 2], 256 * k
                mms = []
                for z in (0, 1):
                    mms += diff(64, pb, 64 * z, f0, S_(y + 128 * z, y + 128 * z + 64), S_(y + 128 * z + 64, y + 128 * z + 128))
                mms += diff(128, pb, 128, f0, S_(y, y + 256, 2), S_(y + 1, y + 256, 2))
                P(mms, ((f0, y, y + 256),) + eye, (bank[pb],))
                absop(d0, y, pb, 0, 256)
            V(64, cp("win", S_(bs, bs + 64), ch, S_(cb, cb + 64)), (chr_,), (bslot,))
            names(0, 1024)
            f1, d1 = B("f1"), B("d1")
            gather(f1, B("o0"), 0, 64, G1, WINS[0])
            for k in (0, 1):
                pb, mms = (PA, PB)[k], []
                for z in (0, 1):
                    y = 512 * k + 256 * z
                    mms += diff(64, pb, 64 * z, f1, S_(y, y + 64), S_(y + 64, y + 128))
                    mms += diff(64, pb, 128 + 64 * z, f1, S_(y + 128, y + 256, 2), S_(y + 129, y + 256, 2))
                P(mms, ((f1, 512 * k, 512 * k + 512),) + eye, (bank[pb],))
                absop(d1, 256 * k, pb, 0, 256)
            names(1, 512)
            f2, d2 = B("f2"), B("d2")
            gather(f2, B("o1"), 0, 32, G2, WINS[1])
            for k in (0, 1):
                y = 256 * k
                P(diff(64, PA, 64 * k, f2, S_(y, y + 64), S_(y + 64, y + 128)) +
                  diff(64, PA, 128 + 64 * k, f2, S_(y + 128, y + 256, 2), S_(y + 129, y + 256, 2)),
                  ((f2, y, y + 256),) + eye, ((PA, 256 * k, 256 * k + 256),))
            absop(d2, 0, PA, 0, 256)
            names(2, 256)
            f3, d3 = B("f3"), B("d3")
            gather(f3, B("o2"), 0, 16, G3, WINS[2])
            P(diff(64, PB, 0, f3, S_(0, 64), S_(64, 128)), ((f3, 0, 128),) + eye, ((PB, 0, 64),))
            P(diff(64, PB, 64, f3, S_(128, 256, 2), S_(129, 256, 2)), ((f3, 128, 256),) + eye, ((PB, 64, 128),))
            absop(d3, 0, PB, 0, 128)
            names(3, 128)
            w4 = B("w4")
            gather(w4, B("o3"), 0, 8, G4, WINS[3])
            mms = []
            for b in range(4):
                mms.append(mm(16, PA, S_(b, 64, 4), "idn", al, w4, S_(16 * b, 16 * b + 16), True, False))
                mms.append(mm(16, PA, S_(b, 64, 4), "nid", al, w4, S_(64 + b, 128, 4), False, True))
            P(mms, (full(w4),) + eye, (bank[PA],))
            dw = B("dw")
            absop(dw, 0, PA, 0, 64)
            nd = 4 + 4 * h
            mms = []
            rd = [full(w4), full("wb8"), full("q8"), full("idn"), full("lt")]
            if h:
                mms.append(mm(4, PB, S_(0, 4), "wb8", al, "w4h0", S_(0, 64, 16), True, True))
                rd.append(full("w4h0"))
            mms.append(mm(4, PB, S_(nd - 4, nd), "wb8", al, w4, S_(0, 64, 16), True, False))
            mms.append(mm(4, PB, S_(nd - 4, nd), "idn", al, "lt", al, False, True))
            for b in range(4):
                mms.append(mm(1, PB, S_(nd, nd + 1), "q8", S_(3 - b, 131 - b), w4, S_(16 * b, 16 * b + 1), b == 0, b == 3))
            P(mms, tuple(rd), (bank[PB],))
            mms = []
            for b in range(4):
                mms.append(mm(16, PS, S_(b, 64, 4), "ob", al, w4, S_(16 * b, 16 * b + 16), True, True))
            for b in range(4):
                mms.append(mm(16, PS, S_(64 + b, 128, 4), "ob", al, w4, S_(16 * b, 16 * b + 16), True, False))
                mms.append(mm(16, PS, S_(64 + b, 128, 4), "nob", al, w4, S_(64 + b, 128, 4), False, True))
            P(mms, (full(w4), full("ob"), full("nob")), (bank[PS],))
            P([mm(64, PT, S_(0, 64), "no16", al, "rhi", al, True, False),
               mm(64, PT, S_(0, 64), "nob", al, "rlo", al, False, False)],
              (full("no16"), full("nob"), full("rhi"), full("rlo")), (bank[PT],))
            P([mm(64, PT, S_(0, 64), "ob", al, dw, al, False, True)], (full("ob"), full(dw)), (bank[PT],))
            rr, ff = B("rr"), B("ff")
            nn = S_(0, nd + 1)
            V(nd, ts(rr, nn, PB, nn, -0.46875, None, AO.add), (bank[PB],), (full(rr),))
            V(nd, tt(ff, nn, PB, nn, rr, nn, AO.subtract), (bank[PB], full(rr)), (full(ff),))
            ds, de, eq, us, t2, s1n, oc = [B(x) for x in ("ds", "de", "eq", "us", "tt", "s1", "oc")]
            own = col(ff, nd)
            A(1, lambda g, T, ds=ds, ff=ff, nd=nd, h=h: g.scalar.activation(
                T[ds][:], T[ff][:, nd:nd + 1], AF.Copy, bias=64.0 * h, scale=128.0), (full(ff),), (full(ds),))
            A(1, lambda g, T, de=de, ff=ff, nd=nd, h=h: g.scalar.activation(
                T[de][:], T[ff][:, nd:nd + 1], AF.Identity, bias=T["kc"][:, h:h + 1], scale=-128.0),
              (full(ff), full("kc")), (full(de),))
            V(nd, ts(eq, S_(0, nd), ff, S_(0, nd), own, None, AO.is_equal), (full(ff),), (full(eq),))
            V(nd, lambda g, T, us=us, eq=eq, nd=nd: g.vector.tensor_reduce(T[us][:], T[eq][:, 0:nd], AxisListType.X, AO.max),
              (full(eq),), (full(us),))
            V(1, ts(t2, al, us, al, col(de, 0), col(ds, 0), AO.mult, AO.add), (full(us), full(de), full(ds)), (full(t2),))
            V(1, ts(s1n, al, us, al, 3.0, 1.0, AO.mult, AO.add), (full(us),), (full(s1n),))
            V(4, ts(oc, al, "pcon", al, col(s1n, 0), col(t2, 0), AO.mult, AO.add), (full("pcon"), full(s1n), full(t2)), (full(oc),))
            gc = B("gc")
            add("a", 65 + 100 * CY, lambda g, T, gc=gc, oc=oc, wlo=wlo, whi=whi: g.scalar.activation(
                T[gc][:], T["win"][:, wlo:whi].indirect(T[oc][:]), AF.Copy), (("win", wlo, whi), full(oc)), (full(gc),))
            ai, am, a3, qq, mc, mr = [B(x) for x in ("ai", "am", "a3", "qq", "mc", "mr")]
            V(64, cp(ai, al, PS, S_(0, 64)), (bank[PS],), (full(ai),))
            A(64, lambda g, T, PS=PS: g.scalar.activation(T[PS][:, 128:192], T[PS][:, 64:128], AF.Relu, scale=8192.0),
              (bank[PS],), (bank[PS],))
            cw = S_(128, 192)
            V(64, ts(am, al, ai, al, 15, None, AO.bitwise_and), (full(ai),), (full(am),))
            V(64, tt(a3, al, am, al, PS, cw, AO.add), (full(am), bank[PS]), (full(a3),))
            V(64, tt(mc, al, PT, S_(0, 64), a3, al, AO.is_gt), (bank[PT], full(a3)), (full(mc),))
            V(64, tt(qq, al, PT, S_(0, 64), am, al, AO.is_gt), (bank[PT], full(am)), (full(qq),))
            V(64, tt(mr, al, qq, al, PS, cw, AO.min), (full(qq), bank[PS]), (full(mr),))
            P([mm(4, PA, S_(0, 4), "p16", S_(15 - r, 143 - r), mc, S_(4 * r, 4 * r + 4), r == 0, r == 15) for r in range(16)],
              (full("p16"), full(mc)), (bank[PA],))
            ee, me = B("ee"), B("me")
            V(64, tt(ee, al, gc, al, "win", S_(bs, bs + 64), AO.subtract), (full(gc), bslot), (full(ee),), 2.0)
            for b in range(4):
                x = 64 + 16 * b
                V(16, ts(PT, S_(64 + b, 128, 4), mr, S_(b, 64, 4), col(PA, b), None, AO.not_equal), (full(mr), bank[PA]), ((PT, x, x + 16),))
            V(64, tt(me, al, PT, S_(64, 128), ee, al, AO.mult), ((PT, 64, 128), full(ee)), (full(me),))
            if t < R - 1:
                bn2, co = B("bn2"), B("co")
                V(64, tt(bn2, al, "win", S_(bs, bs + 64), me, al, AO.add), (bslot, full(me)), (full(bn2),), 2.0)
                V(64, cp(co, S_(cb, cb + 64), bn2, al), (full(bn2),), ((co, cb, cb + 64),))
                sends[(t, h)] = add("g", 500.0, ("send", t, h), ((co, cb, cb + 64),), ())
            else:
                for b in range(4):
                    x = 64 * h + 16 * b
                    V(16, tt("ybt", S_(x, x + 16), "win", S_(bs + b, bs + 64, 4), me, S_(b, 64, 4), AO.add),
                      (bslot, full(me)), (("ybt", x, x + 16),), 2.0)
                D("s", "sb%d" % h, lambda T, h=h: T.yb[:, 64 * h:64 * h + 64], lambda T, h=h: T.ybt[:, 64 * h:64 * h + 64],
                  2000.0, (("ybt", 64 * h, 64 * h + 64),), ())
            add("v", 50 + 64 * 3.0 * CY, lambda g, T, gc=gc, me=me, oc=oc, wlo=wlo, whi=whi: g.vector.tensor_tensor(
                T["win"][:, wlo:whi].indirect(T[oc][:]), T[gc][:], T[me][:], AO.subtract),
                (full(gc), full(me), full(oc)), (("win", wlo, whi),))
            qs = B("qs")
            if t == 0:
                V(64, cp(qs, al, qq, al), (full(qq),), (full(qs),), 0.5)
            else:
                V(64, tt(qs, al, qs, al, qq, al, AO.add), (full(qs), full(qq)), (full(qs),), 2.0)
            if t == R - 1:
                P([mm(4, PT, S_(0, 4), "p16", S_(15 - r, 143 - r), qs, S_(4 * r, 4 * r + 4), r == 0, r == 15) for r in range(16)],
                  (full("p16"), full(qs)), (bank[PT],))
                V(4, cp("yqt", S_(4 * h, 4 * h + 4), PT, S_(0, 4)), (bank[PT],), (("yqt", 4 * h, 4 * h + 4),))
    cur[0] = 0
    D("s", "sq", lambda T: T.yq[:], lambda T: T.yqt[:], 2000.0, (full("yqt"),), ())
    D("s", "sc", lambda T: T.yc[:], lambda T: T.win[:, 64:192], 2000.0, (("win", 64, 192),), ())
    return ops


def schedule(ops):
    n = len(ops)
    succ = [[] for _ in range(n)]

    def lat(j, i):
        if j in ops[i]["late"]:
            return HOP
        if ops[j]["eng"] == ops[i]["eng"] and ops[j]["sem"] is None:
            return SAME if j in ops[i]["waits"] else 0.0
        return ops[j]["tail"] + WAKE
    for i in range(n):
        for j in ops[i]["order"]:
            succ[j].append(i)
    pr = [0.0] * n
    for i in range(n - 1, -1, -1):
        pr[i] = ops[i]["dur"] + max([ops[i]["tail"]] + [lat(i, k) + pr[k] for k in succ[i]])
    key = [pr[i] - SECOND * ops[i]["h"] for i in range(n)]
    left = [len(o["order"]) for o in ops]
    ready = [0.0] * n
    avail = {}
    for i in range(n):
        if not left[i]:
            avail.setdefault(ops[i]["eng"], []).append(i)
    free, out, start, end = {}, [], [0.0] * n, [0.0] * n
    while any(avail.values()):
        best = None
        for e, l in avail.items():
            if not l:
                continue
            t = max(free.get(e, 0.0), min(ready[i] for i in l))
            i = max((x for x in l if ready[x] <= t + 20.0), key=lambda x: (key[x], -x))
            t = max(t, ready[i])
            if best is None or t < best[0]:
                best = (t, i, e)
        t, i, e = best
        avail[e].remove(i)
        start[i], end[i] = t, t + ops[i]["dur"]
        free[e] = end[i]
        out.append(i)
        for k in succ[i]:
            ready[k] = max(ready[k], end[i] + lat(i, k))
            left[k] -= 1
            if not left[k]:
                avail.setdefault(ops[k]["eng"], []).append(k)
    return out, start, end


_plan = []


def plan():
    if not _plan:
        ops = build()
        order, start, end = schedule(ops)
        cnt, pos, known, clock, wl = {}, {}, {}, {}, {}
        for i in order:
            o = ops[i]
            e = o["eng"]
            kn = known.setdefault(e, {})
            w = []
            for j in sorted(o["waits"], key=lambda x: -start[x]):
                s, v = pos[j]
                if kn.get(s, 0) >= v:
                    continue
                w.append((s, v))
                for s2, v2 in clock[j].items():
                    if kn.get(s2, 0) < v2:
                        kn[s2] = v2
            wl[i] = w
            if o["sem"] is not None:
                pos[i] = o["sem"]
            elif isinstance(o["emit"], tuple):
                pos[i] = None
            else:
                cnt["c" + e] = cnt.get("c" + e, 0) + 1
                pos[i] = ("c" + e, cnt["c" + e])
            c = dict(kn)
            if pos[i]:
                c[pos[i][0]] = pos[i][1]
            clock[i] = c
        _plan.append((ops, order, wl, pos, cnt, start, end))
    return _plan[0]


def relay_of(core, dst, topo):
    ok = [c for c in topo.cores_of(core) if c != core and topo.may_write(c, dst)]
    near = [c for c in ok if topo.die(c) == topo.die(core)]
    return (near or ok)[0]


def mask_of(src, dst, topo):
    return sum(1 << e for e in topo.engines(src, dst)[:NENG])


def rank_program(g, core, T, topo):
    ops, order, wl, pos, cnt, start, end = plan()
    pieces = [ops[i]["emit"][1:] for i in order if isinstance(ops[i]["emit"], tuple)]
    rank = T.rank_of(core)
    if rank is None:
        for q in range(N):
            src, dst = T.cores[q], T.cores[(q + H) % N]
            if relay_of(src, dst, topo) != core:
                continue
            rid, pid = topo.addr(dst, core)
            for t, h in pieces:
                g.wait_ge(T.sem["rl%d%d" % (t + 1, h)], NENG)
                tile = T["chh%d" % h][:, 64 * (t + 1):64 * (t + 2)]
                g.remote_dma(tile, tile, T.sem["ar%d%d" % (t + 1, h)], T.sem.snd, pid, rid, mask_of(core, dst, topo))
            g.wait_ge(T.sem.snd, NENG * len(pieces))
        return
    nxt = T.cores[(rank + H) % N]
    rel = relay_of(core, nxt, topo)
    rid, pid = topo.addr(rel, core)
    queue = {"v": g.vector, "a": g.scalar, "p": g.tensor, "g": g, "s": g.sync}
    for i in order:
        o = ops[i]
        if o["emit"] is None:
            continue
        q = queue[o["eng"]]
        for s, v in wl[i]:
            q.wait_ge(T.sem[s], v)
        if isinstance(o["emit"], tuple):
            t, h = o["emit"][1:]
            g.remote_dma(T["chh%d" % h][:, 64 * (t + 1):64 * (t + 2)], T["coh%d" % h][:, 64 * t:64 * (t + 1)],
                         T.sem["rl%d%d" % (t + 1, h)], T.sem.snd, pid, rid, mask_of(core, rel, topo))
        else:
            o["emit"](g, T).then_inc(T.sem[pos[i][0]], 16 if o["sem"] else 1)
    g.wait_ge(T.sem.snd, NENG * len(pieces))
    for t in range(1, R):
        for h in (0, 1):
            g.wait_ge(T.sem["ar%d%d" % (t, h)], NENG)
    for d in DMAS[:8]:
        g.wait_ge(T.sem["m_" + d], 16)
    for s in ("cg", "cp", "ca", "cv"):
        g.wait_ge(T.sem[s], cnt[s])
    for d in DMAS[8:]:
        g.wait_ge(T.sem["m_" + d], 16)
